import numpy as np
CORES = [0,1,2,3,4,5,6,7,8,9,10,11,12,13,14,15,16,17,18,19,20,21,22,23,24,25,26,27,28,29,30,31,32,33,34,35,36,37,38,39,40,41,42,43,44,45,46,47,48,49,50,51,52,53,54,55,56,57,58,59,60,61,62,63,64,65,66,67,68,69,70,71,72,73,74,75,76,77,78,79,80,81,82,83,84,85,86,87,88,89,90,91,92,93,94,95,96,97,98,99,100,101,102,103,104,105,106,107,108,109,110,111,112,113,114,115,116,117,118,119,120,121,122,123,124,125,126,127,128,129,130,131,132,133,134,135,136,137,138,139,140,141,142,143,144,145,146,147,148,149,150,151,152,153,154,155,156,157,158,159,160,161,162,163,164,165,166,167,168,169,170,171,172,173,174,175,176,177,178,179,180,181,182,183,184,185,186,187,188,189,190,191,192,193,194,195,196,197,198,199,200,201,202,203,204,205,206,207,208,209,210,211,212,213,214,215,216,217,218,219,220,221,222,223,224,225,226,227,228,229,230,231,232,233,234,235,236,237,238,239,240,241,242,243,244,245,246,247,248,249,250,251,252,253,254,255,256,257,258,259,260,261,262,263,264,265,266,267,268,269,270,271,272,273,274,275,276,277,278,279,280,281,282,283,284,285,286,287,288,289,290,291,292,293,294,295,296,297,298,299,300,301,302,303,304,305,306,307,308,309,310,311,312,313,314,315,316,317,318,319,320,321,322,323,324,325,326,327,328,329,330,331,332,333,334,335,336,337,338,339,340,341,342,343,344,345,346,347,348,349,350,351,352,353,354,355,356,357,358,359,360,361,362,363,364,365,366,367,368,369,370,371,372,373,374,375,376,377,378,379,380,381,382,383,384,385,386,387,388,389,390,391,392,393,394,395,396,397,398,399,400,401,402,403,404,405,406,407,408,409,410,411,412,413,414,415,416,417,418,419,420,421,422,423,424,425,426,427,428,429,430,431,432,433,434,435,436,437,438,439,440,441,442,443,444,445,446,447,448,449,450,451,452,453,454,455,456,457,458,459,460,461,462,463,464,465,466,467,468,469,470,471,472,473,474,475,476,477,478,479,480,481,482,483,484,485,486,487,488,489,490,491,492,493,494,495,496,497,498,499,500,501,502,503,504,505,506,507,508,509,510,511]
N = 512
ROOT = 219
def setup_inputs(rng):
    return {"x": rng.standard_normal((N, 128, 512), dtype=np.float32)}
def reference(x):
    return {"y": np.broadcast_to(x[ROOT], x.shape)}

@@ -1,0 +1,66 @@
+from concourse.bass import RemoteDMATransfer, DstId
+
+SCRATCH = {
+    "land": ("sbuf", [128, 512], "float32"),
+}
+SEMAPHORES = ["loaded", "sent", "arrived", "stored"]
+
+ROOT = 219
+
+
+def build_tree():
+    lead = lambda h, c: h * 128 + c * 8 + 3
+    children = {}
+    cap = {}
+    for h in range(4):
+        for c in range(16):
+            children[lead(h, c)] = []
+            cap[lead(h, c)] = 3
+    def link(a, b):
+        children[a].append(b)
+        cap[a] -= 1
+    link(lead(1, 11), lead(0, 11))
+    link(lead(1, 11), lead(2, 11))
+    link(lead(2, 11), lead(3, 11))
+    for h in range(4):
+        queue = [lead(h, 11)]
+        todo = [lead(h, c) for c in range(16) if c != 11]
+        while todo:
+            a = queue.pop(0)
+            while cap[a] > 0 and todo:
+                b = todo.pop(0)
+                link(a, b)
+                queue.append(b)
+    return children
+
+
+def rank_program(g, core, T, topo):
+    children = build_tree()
+    buf = T.land[:]
+    leader = core - core % 8 + 3
+    sent = 0
+    if core == ROOT:
+        g.dma_start(buf, T.x[:]).then_inc(T.sem.loaded, 16)
+        g.wait_ge(T.sem.loaded, 16)
+    elif core == leader:
+        g.wait_ge(T.sem.arrived, 8)
+    else:
+        g.wait_ge(T.sem.arrived, 16)
+    if core == leader:
+        kids = children[core]
+        if kids:
+            ids = [topo.addr(d, core) for d in kids]
+            g.remote_dma_fused([RemoteDMATransfer(dst_ids=[DstId(rid=r, pnc=p) for r, p in ids], dma_engine_mask=0xFF,
+                                                  remote_sem=T.sem.arrived, srcs=[buf], dsts=[buf for _d in kids])],
+                               local_sem=T.sem.sent)
+            sent += 8
+        mine = [d for d in range(core - 3, core + 5) if d != core]
+        ids = [topo.addr(d, core) for d in mine]
+        g.remote_dma_fused([RemoteDMATransfer(dst_ids=[DstId(rid=r, pnc=p) for r, p in ids], dma_engine_mask=0xFFFF,
+                                              remote_sem=T.sem.arrived, srcs=[buf], dsts=[buf for _d in mine])],
+                           local_sem=T.sem.sent)
+        sent += 16
+    g.dma_start(T.y[:], buf).then_inc(T.sem.stored, 16)
+    g.wait_ge(T.sem.stored, 16)
+    if sent:
+        g.wait_ge(T.sem.sent, sent)

@@ -1,66 +1,219 @@
 from concourse.bass import RemoteDMATransfer, DstId
 
+NUNITS = 32
 SCRATCH = {
-    "land": ("sbuf", [128, 512], "float32"),
+    "xs": ("dram", [NUNITS, 128, 16], "float32"),
 }
-SEMAPHORES = ["loaded", "sent", "arrived", "stored"]
+SEMAPHORES = ["s1", "s2", "s3", "s4", "s5", "s6", "s7", "sent", "loaded", "stored"]
 
 ROOT = 219
+ROOT_HOST, ROOT_K, ROOT_P = 1, 5, 1
+HOST_CHAIN = [1, 0, 3, 2]
+CACHE = {}
+
+TREES = {
+    0: [((5, 1), (0, 0)), ((0, 0), "H0"), ((0, 0), (3, 0)), ((3, 0), (1, 1)), ((3, 0), (4, 1)), ((4, 1), (6, 0)),
+        ((4, 1), (2, 1)), ((1, 1), (3, 1)), ((1, 1), (1, 0)), ((6, 0), (0, 1)), ((6, 0), (4, 0)), ((2, 1), (2, 0)),
+        ((2, 1), (7, 1)), ((1, 0), (7, 0)), ((1, 0), (6, 1)), ((3, 1), (5, 0))],
+    1: [((5, 1), (7, 1)), ((7, 1), "H0"), ((7, 1), (7, 0)), ((7, 0), (5, 0)), ((7, 0), (0, 1)), ((5, 0), (2, 0)),
+        ((5, 0), (6, 1)), ((0, 1), (4, 0)), ((0, 1), (3, 1)), ((4, 0), (0, 0)), ((4, 0), (1, 1)), ((2, 0), (1, 0)),
+        ((2, 0), (2, 1)), ((6, 1), (3, 0)), ((6, 1), (4, 1)), ((3, 1), (6, 0))],
+}
 
 
-def build_tree():
-    lead = lambda h, c: h * 128 + c * 8 + 3
-    children = {}
-    cap = {}
+def cid(h, k, p, c):
+    return h * 128 + (2 * k + p) * 8 + c
+
+
+def unit(k, p, e):
+    return p * 16 + e * 8 + k
+
+
+def chip_of(core):
+    return core // 8
+
+
+def build_edges():
+    depth = {}
+    sends = []
+
+    def send(u, src, dsts):
+        d = depth[(u, src)] + 1
+        for t in dsts:
+            assert (u, t) not in depth, (u, src, t)
+            depth[(u, t)] = d
+        sends.append((u, src, list(dsts), d))
+
+    for u in range(NUNITS):
+        depth[(u, ROOT)] = 0
+
+    chips = [(k, p) for p in (0, 1) for k in range(8)]
+    rchip = (ROOT_K, ROOT_P)
+
+    def is_root_chip(h, k, p):
+        return (h, k, p) == (ROOT_HOST, ROOT_K, ROOT_P)
+
+    def home(h, k, p, e):
+        return cid(h, k, p, 4 * e + 2)
+
+    def others_on_chip(core):
+        base = core - core % 8
+        return [c for c in range(base, base + 8) if c != core]
+
+    land = {}
     for h in range(4):
-        for c in range(16):
-            children[lead(h, c)] = []
-            cap[lead(h, c)] = 3
-    def link(a, b):
-        children[a].append(b)
-        cap[a] -= 1
-    link(lead(1, 11), lead(0, 11))
-    link(lead(1, 11), lead(2, 11))
-    link(lead(2, 11), lead(3, 11))
-    for h in range(4):
-        queue = [lead(h, 11)]
-        todo = [lead(h, c) for c in range(16) if c != 11]
-        while todo:
-            a = queue.pop(0)
-            while cap[a] > 0 and todo:
-                b = todo.pop(0)
-                link(a, b)
-                queue.append(b)
-    return children
+        for (k, p) in chips:
+            if is_root_chip(h, k, p):
+                continue
+            table = {}
+            for e in (0, 1):
+                foreign = [unit(k2, p2, e) for (k2, p2) in chips if (k2, p2) != (k, p)]
+                if h == ROOT_HOST:
+                    xu = unit(ROOT_K, ROOT_P, e)
+                    foreign = [xu] + [f for f in foreign if f != xu]
+                seats = [2, 2, 3, 3, 3, 3, 3, 0, 0, 0, 0, 1, 1, 1, 1]
+                for f, c in zip(foreign, seats):
+                    table[f] = cid(h, k, p, 4 * e + c)
+            land[(h, k, p)] = table
+
+    def first_stop(k, p, e):
+        if (k, p) != rchip:
+            return home(ROOT_HOST, k, p, e)
+        k2, p2 = TREES[e][0][1]
+        return home(ROOT_HOST, k2, p2, e)
+
+    def rc(c):
+        return cid(ROOT_HOST, ROOT_K, ROOT_P, c)
+
+    sibs = [rc(c) for c in range(8) if rc(c) != ROOT]
+    kk = [k for k in range(8) if k != ROOT_K]
+    full = {
+        0: [(k, 1, 0) for k in kk[:4]],
+        1: [(k, 1, 0) for k in kk[4:]],
+        4: [(k, 1, 1) for k in kk[:4]],
+        5: [(k, 1, 1) for k in kk[4:]] + [(ROOT_K, 1, 1)],
+        6: [(k, 0, 1) for k in range(4)],
+        7: [(k, 0, 1) for k in range(4, 8)],
+        2: [(k, 0, 0) for k in range(4)],
+    }
+    passed = [((4, 0, 0), 0), ((5, 0, 0), 4), ((6, 0, 0), 5)]
+    direct = [((7, 0, 0), 1), ((ROOT_K, 1, 0), 1)]
+    for c, us in full.items():
+        for kpe in us:
+            send(unit(*kpe), ROOT, [rc(c)])
+    for (kpe, w) in passed:
+        send(unit(*kpe), ROOT, [rc(2)])
+    for (kpe, w) in direct:
+        send(unit(*kpe), ROOT, [rc(w), first_stop(*kpe)])
+    for c, us in full.items():
+        for kpe in us:
+            send(unit(*kpe), rc(c), [s for s in sibs if s != rc(c)] + [first_stop(*kpe)])
+    for (kpe, w) in passed:
+        send(unit(*kpe), rc(2), [rc(w), first_stop(*kpe)])
+    for (kpe, w) in passed:
+        send(unit(*kpe), rc(w), [s for s in sibs if s not in (rc(w), rc(2))])
+    for (kpe, w) in direct:
+        send(unit(*kpe), rc(w), [s for s in sibs if s != rc(w)])
+
+    for e in (0, 1):
+        xu = unit(ROOT_K, ROOT_P, e)
+        for node in [b for (a, b) in TREES[e] if b != "H0"]:
+            out = []
+            for (a, b) in TREES[e]:
+                if a == node:
+                    out.append(home(HOST_CHAIN[1], ROOT_K, ROOT_P, e) if b == "H0" else home(ROOT_HOST, b[0], b[1], e))
+            src = home(ROOT_HOST, node[0], node[1], e)
+            send(xu, src, others_on_chip(src) + out)
+
+    for i, h in enumerate(HOST_CHAIN):
+        for (k, p) in chips:
+            if is_root_chip(h, k, p):
+                continue
+            for e in (0, 1):
+                u = unit(k, p, e)
+                out = [land[(h, k2, p2)][u] for (k2, p2) in chips if (k2, p2) != (k, p) and not is_root_chip(h, k2, p2)]
+                if i + 1 < len(HOST_CHAIN):
+                    out.append(home(HOST_CHAIN[i + 1], k, p, e))
+                send(u, home(h, k, p, e), out + [cid(h, k, p, 4 * e + 0)])
+    for h in HOST_CHAIN:
+        for (k, p) in chips:
+            if is_root_chip(h, k, p):
+                continue
+            for e in (0, 1):
+                helper = cid(h, k, p, 4 * e + 0)
+                send(unit(k, p, e), helper, [c for c in others_on_chip(helper) if c != home(h, k, p, e)])
+            for u, core in sorted(land[(h, k, p)].items()):
+                if h == ROOT_HOST and u in (unit(ROOT_K, ROOT_P, 0), unit(ROOT_K, ROOT_P, 1)):
+                    continue
+                send(u, core, others_on_chip(core))
+    return sends, depth
+
+
+def build_plan():
+    if "plan" in CACHE:
+        return CACHE["plan"]
+    sends, depth = build_edges()
+    per = {}
+    for (u, src, dsts, d) in sends:
+        lst = per.setdefault(src, {}).setdefault(d, [])
+        for i in range(0, len(dsts), 16):
+            lst.append((u, dsts[i:i + 16]))
+    calls, expect, sent = {}, {}, {}
+    for src, by_depth in per.items():
+        calls[src] = {}
+        for d, trs in by_depth.items():
+            trs = sorted(trs, key=lambda t: 0 if any(chip_of(x) != chip_of(src) for x in t[1]) else 1)
+            out = []
+            ncalls = (len(trs) + 15) // 16
+            for ci in range(ncalls):
+                part = trs[ci::ncalls]
+                off = any(chip_of(x) != chip_of(src) for t in part for x in t[1])
+                n = (8 if off and len(part) <= 8 else 16) // len(part)
+                while n & (n - 1):
+                    n -= 1
+                call = []
+                for j, (u, dsts) in enumerate(part):
+                    mask = ((1 << n) - 1) << (j * n)
+                    if any(chip_of(x) != chip_of(src) for x in dsts):
+                        assert mask <= 0xFF
+                    call.append((u, dsts, mask, n))
+                    for x in dsts:
+                        ex = expect.setdefault(x, {})
+                        ex[d] = ex.get(d, 0) + n
+                    sent[src] = sent.get(src, 0) + n
+                out.append(call)
+            calls[src][d] = out
+    CACHE["plan"] = (calls, expect, sent)
+    return CACHE["plan"]
 
 
 def rank_program(g, core, T, topo):
-    children = build_tree()
-    buf = T.land[:]
-    leader = core - core % 8 + 3
-    sent = 0
+    calls, expect, sent = build_plan()
+    sems = {1: T.sem.s1, 2: T.sem.s2, 3: T.sem.s3, 4: T.sem.s4, 5: T.sem.s5, 6: T.sem.s6, 7: T.sem.s7}
+    mine = calls.get(core, {})
+    arrivals = expect.get(core, {})
+    waited = set()
+
+    def wait_below(limit):
+        for d in sorted(arrivals):
+            if d < limit and d not in waited:
+                g.wait_ge(sems[d], arrivals[d])
+                waited.add(d)
+
     if core == ROOT:
-        g.dma_start(buf, T.x[:]).then_inc(T.sem.loaded, 16)
+        g.dma_start(T.xs[:], T.x[:]).then_inc(T.sem.loaded, 16)
         g.wait_ge(T.sem.loaded, 16)
-    elif core == leader:
-        g.wait_ge(T.sem.arrived, 8)
-    else:
-        g.wait_ge(T.sem.arrived, 16)
-    if core == leader:
-        kids = children[core]
-        if kids:
-            ids = [topo.addr(d, core) for d in kids]
-            g.remote_dma_fused([RemoteDMATransfer(dst_ids=[DstId(rid=r, pnc=p) for r, p in ids], dma_engine_mask=0xFF,
-                                                  remote_sem=T.sem.arrived, srcs=[buf], dsts=[buf for _d in kids])],
-                               local_sem=T.sem.sent)
-            sent += 8
-        mine = [d for d in range(core - 3, core + 5) if d != core]
-        ids = [topo.addr(d, core) for d in mine]
-        g.remote_dma_fused([RemoteDMATransfer(dst_ids=[DstId(rid=r, pnc=p) for r, p in ids], dma_engine_mask=0xFFFF,
-                                              remote_sem=T.sem.arrived, srcs=[buf], dsts=[buf for _d in mine])],
-                           local_sem=T.sem.sent)
-        sent += 16
-    g.dma_start(T.y[:], buf).then_inc(T.sem.stored, 16)
+    for d in sorted(mine):
+        wait_below(d)
+        for call in mine[d]:
+            transfers = []
+            for (u, dsts, mask, n) in call:
+                ids = [topo.addr(x, core) for x in dsts]
+                transfers.append(RemoteDMATransfer(dst_ids=[DstId(rid=r, pnc=p) for (r, p) in ids], dma_engine_mask=mask,
+                                                   remote_sem=sems[d], srcs=[T.xs[u]], dsts=[T.xs[u] for x in dsts]))
+            g.remote_dma_fused(transfers, local_sem=T.sem.sent)
+    wait_below(99)
+    g.dma_start(T.y[:], T.xs[:]).then_inc(T.sem.stored, 16)
     g.wait_ge(T.sem.stored, 16)
-    if sent:
-        g.wait_ge(T.sem.sent, sent)
+    if core in sent:
+        g.wait_ge(T.sem.sent, sent[core])

@@ -96,8 +96,8 @@ def build_edges():
         7: [(k, 0, 1) for k in range(4, 8)],
         2: [(k, 0, 0) for k in range(4)],
     }
-    passed = [((4, 0, 0), 0), ((5, 0, 0), 4), ((6, 0, 0), 5)]
-    direct = [((7, 0, 0), 1), ((ROOT_K, 1, 0), 1)]
+    passed = [((4, 0, 0), 0), ((5, 0, 0), 4), ((ROOT_K, 1, 0), 5)]
+    direct = [((6, 0, 0), 1), ((7, 0, 0), 1)]
     for c, us in full.items():
         for kpe in us:
             send(unit(*kpe), ROOT, [rc(c)])

from concourse.bass import RemoteDMATransfer, DstId

NUNITS = 32
SCRATCH = {
    "xs": ("dram", [NUNITS, 128, 16], "float32"),
}
SEMAPHORES = ["s1", "s2", "s3", "s4", "s5", "s6", "s7", "sent", "loaded", "stored"]

ROOT = 219
ROOT_HOST, ROOT_K, ROOT_P = 1, 5, 1
HOST_CHAIN = [1, 0, 3, 2]
CACHE = {}

TREES = {
    0: [((5, 1), (0, 0)), ((0, 0), "H0"), ((0, 0), (3, 0)), ((3, 0), (1, 1)), ((3, 0), (4, 1)), ((4, 1), (6, 0)),
        ((4, 1), (2, 1)), ((1, 1), (3, 1)), ((1, 1), (1, 0)), ((6, 0), (0, 1)), ((6, 0), (4, 0)), ((2, 1), (2, 0)),
        ((2, 1), (7, 1)), ((1, 0), (7, 0)), ((1, 0), (6, 1)), ((3, 1), (5, 0))],
    1: [((5, 1), (7, 1)), ((7, 1), "H0"), ((7, 1), (7, 0)), ((7, 0), (5, 0)), ((7, 0), (0, 1)), ((5, 0), (2, 0)),
        ((5, 0), (6, 1)), ((0, 1), (4, 0)), ((0, 1), (3, 1)), ((4, 0), (0, 0)), ((4, 0), (1, 1)), ((2, 0), (1, 0)),
        ((2, 0), (2, 1)), ((6, 1), (3, 0)), ((6, 1), (4, 1)), ((3, 1), (6, 0))],
}


def cid(h, k, p, c):
    return h * 128 + (2 * k + p) * 8 + c


def unit(k, p, e):
    return p * 16 + e * 8 + k


def chip_of(core):
    return core // 8


def build_edges():
    depth = {}
    sends = []

    def send(u, src, dsts):
        d = depth[(u, src)] + 1
        for t in dsts:
            assert (u, t) not in depth, (u, src, t)
            depth[(u, t)] = d
        sends.append((u, src, list(dsts), d))

    for u in range(NUNITS):
        depth[(u, ROOT)] = 0

    chips = [(k, p) for p in (0, 1) for k in range(8)]
    rchip = (ROOT_K, ROOT_P)

    def is_root_chip(h, k, p):
        return (h, k, p) == (ROOT_HOST, ROOT_K, ROOT_P)

    def home(h, k, p, e):
        return cid(h, k, p, 4 * e + 2)

    def others_on_chip(core):
        base = core - core % 8
        return [c for c in range(base, base + 8) if c != core]

    land = {}
    for h in range(4):
        for (k, p) in chips:
            if is_root_chip(h, k, p):
                continue
            table = {}
            for e in (0, 1):
                foreign = [unit(k2, p2, e) for (k2, p2) in chips if (k2, p2) != (k, p)]
                if h == ROOT_HOST:
                    xu = unit(ROOT_K, ROOT_P, e)
                    foreign = [xu] + [f for f in foreign if f != xu]
                seats = [2, 2, 3, 3, 3, 3, 3, 0, 0, 0, 0, 1, 1, 1, 1]
                for f, c in zip(foreign, seats):
                    table[f] = cid(h, k, p, 4 * e + c)
            land[(h, k, p)] = table

    def first_stop(k, p, e):
        if (k, p) != rchip:
            return home(ROOT_HOST, k, p, e)
        k2, p2 = TREES[e][0][1]
        return home(ROOT_HOST, k2, p2, e)

    def rc(c):
        return cid(ROOT_HOST, ROOT_K, ROOT_P, c)

    sibs = [rc(c) for c in range(8) if rc(c) != ROOT]
    kk = [k for k in range(8) if k != ROOT_K]
    full = {
        0: [(k, 1, 0) for k in kk[:4]],
        1: [(k, 1, 0) for k in kk[4:]],
        4: [(k, 1, 1) for k in kk[:4]],
        5: [(k, 1, 1) for k in kk[4:]] + [(ROOT_K, 1, 1)],
        6: [(k, 0, 1) for k in range(4)],
        7: [(k, 0, 1) for k in range(4, 8)],
        2: [(k, 0, 0) for k in range(4)],
    }
    passed = [((4, 0, 0), 0), ((5, 0, 0), 4), ((ROOT_K, 1, 0), 5)]
    direct = [((6, 0, 0), 1), ((7, 0, 0), 1)]
    for c, us in full.items():
        for kpe in us:
            send(unit(*kpe), ROOT, [rc(c)])
    for (kpe, w) in passed:
        send(unit(*kpe), ROOT, [rc(2)])
    for (kpe, w) in direct:
        send(unit(*kpe), ROOT, [rc(w), first_stop(*kpe)])
    for c, us in full.items():
        for kpe in us:
            send(unit(*kpe), rc(c), [s for s in sibs if s != rc(c)] + [first_stop(*kpe)])
    for (kpe, w) in passed:
        send(unit(*kpe), rc(2), [rc(w), first_stop(*kpe)])
    for (kpe, w) in passed:
        send(unit(*kpe), rc(w), [s for s in sibs if s not in (rc(w), rc(2))])
    for (kpe, w) in direct:
        send(unit(*kpe), rc(w), [s for s in sibs if s != rc(w)])

    for e in (0, 1):
        xu = unit(ROOT_K, ROOT_P, e)
        for node in [b for (a, b) in TREES[e] if b != "H0"]:
            out = []
            for (a, b) in TREES[e]:
                if a == node:
                    out.append(home(HOST_CHAIN[1], ROOT_K, ROOT_P, e) if b == "H0" else home(ROOT_HOST, b[0], b[1], e))
            src = home(ROOT_HOST, node[0], node[1], e)
            send(xu, src, others_on_chip(src) + out)

    for i, h in enumerate(HOST_CHAIN):
        for (k, p) in chips:
            if is_root_chip(h, k, p):
                continue
            for e in (0, 1):
                u = unit(k, p, e)
                out = [land[(h, k2, p2)][u] for (k2, p2) in chips if (k2, p2) != (k, p) and not is_root_chip(h, k2, p2)]
                if i + 1 < len(HOST_CHAIN):
                    out.append(home(HOST_CHAIN[i + 1], k, p, e))
                send(u, home(h, k, p, e), out + [cid(h, k, p, 4 * e + 0)])
    for h in HOST_CHAIN:
        for (k, p) in chips:
            if is_root_chip(h, k, p):
                continue
            for e in (0, 1):
                helper = cid(h, k, p, 4 * e + 0)
                send(unit(k, p, e), helper, [c for c in others_on_chip(helper) if c != home(h, k, p, e)])
            for u, core in sorted(land[(h, k, p)].items()):
                if h == ROOT_HOST and u in (unit(ROOT_K, ROOT_P, 0), unit(ROOT_K, ROOT_P, 1)):
                    continue
                send(u, core, others_on_chip(core))
    return sends, depth


def build_plan():
    if "plan" in CACHE:
        return CACHE["plan"]
    sends, depth = build_edges()
    per = {}
    for (u, src, dsts, d) in sends:
        lst = per.setdefault(src, {}).setdefault(d, [])
        for i in range(0, len(dsts), 16):
            lst.append((u, dsts[i:i + 16]))
    calls, expect, sent = {}, {}, {}
    for src, by_depth in per.items():
        calls[src] = {}
        for d, trs in by_depth.items():
            trs = sorted(trs, key=lambda t: 0 if any(chip_of(x) != chip_of(src) for x in t[1]) else 1)
            out = []
            ncalls = (len(trs) + 15) // 16
            for ci in range(ncalls):
                part = trs[ci::ncalls]
                off = any(chip_of(x) != chip_of(src) for t in part for x in t[1])
                n = (8 if off and len(part) <= 8 else 16) // len(part)
                while n & (n - 1):
                    n -= 1
                call = []
                for j, (u, dsts) in enumerate(part):
                    mask = ((1 << n) - 1) << (j * n)
                    if any(chip_of(x) != chip_of(src) for x in dsts):
                        assert mask <= 0xFF
                    call.append((u, dsts, mask, n))
                    for x in dsts:
                        ex = expect.setdefault(x, {})
                        ex[d] = ex.get(d, 0) + n
                    sent[src] = sent.get(src, 0) + n
                out.append(call)
            calls[src][d] = out
    CACHE["plan"] = (calls, expect, sent)
    return CACHE["plan"]


def rank_program(g, core, T, topo):
    calls, expect, sent = build_plan()
    sems = {1: T.sem.s1, 2: T.sem.s2, 3: T.sem.s3, 4: T.sem.s4, 5: T.sem.s5, 6: T.sem.s6, 7: T.sem.s7}
    mine = calls.get(core, {})
    arrivals = expect.get(core, {})
    waited = set()

    def wait_below(limit):
        for d in sorted(arrivals):
            if d < limit and d not in waited:
                g.wait_ge(sems[d], arrivals[d])
                waited.add(d)

    if core == ROOT:
        g.dma_start(T.xs[:], T.x[:]).then_inc(T.sem.loaded, 16)
        g.wait_ge(T.sem.loaded, 16)
    for d in sorted(mine):
        wait_below(d)
        for call in mine[d]:
            transfers = []
            for (u, dsts, mask, n) in call:
                ids = [topo.addr(x, core) for x in dsts]
                transfers.append(RemoteDMATransfer(dst_ids=[DstId(rid=r, pnc=p) for (r, p) in ids], dma_engine_mask=mask,
                                                   remote_sem=sems[d], srcs=[T.xs[u]], dsts=[T.xs[u] for x in dsts]))
            g.remote_dma_fused(transfers, local_sem=T.sem.sent)
    wait_below(99)
    g.dma_start(T.y[:], T.xs[:]).then_inc(T.sem.stored, 16)
    g.wait_ge(T.sem.stored, 16)
    if core in sent:
        g.wait_ge(T.sem.sent, sent[core])
